import numpy as np
import ml_dtypes


def mxq(x, axis, fmt="e4m3"):
    dtype, down = {"e4m3": (ml_dtypes.float8_e4m3fn, 7), "e5m2": (ml_dtypes.float8_e5m2, 14)}[fmt]
    v = np.moveaxis(np.asarray(x, np.float32).astype(ml_dtypes.bfloat16).astype(np.float64), axis, -1)
    blocks = v.reshape(v.shape[:-1] + (-1, 32))
    amax = np.abs(blocks).max(-1, keepdims=True)
    byte = np.maximum(np.where(amax > 0, np.frexp(amax)[1] - 1 + 127, 0) - down, 1)
    scale = np.exp2(byte - 127.0)
    codes = (blocks / scale).astype(np.float32).astype(dtype).astype(np.float64)
    return np.moveaxis((codes * scale).reshape(v.shape), -1, axis)


WIDE = False


def mx_kscale(k):
    if not WIDE:
        return np.ones(k)
    levels = np.array([10, -10, 5, -5, 0])
    if k % 512:
        return np.exp2(np.random.permutation(np.resize(levels, k // 32))).repeat(32)
    a = np.empty((k // 512, 16))
    for p in range(k // 512):
        a[p, :8] = np.random.permutation(np.resize(levels, 8))
        for g in range(8):
            far = levels[np.abs(levels - a[p, g]) >= 10]
            a[p, g + 8] = far[np.random.randint(len(far))]
    return np.exp2(a.ravel()).repeat(32)


def f64(x):
    return np.asarray(x).astype(np.float64)


def striped(idx):
    return np.tile(np.asarray(idx).reshape(-1, 16).T, (8, 1)).astype(np.uint16)


def unstriped(offs):
    return offs[:16].T.reshape(-1).astype(np.int64)


E2M1 = np.array([0.0, 0.5, 1.0, 1.5, 2.0, 3.0, 4.0, 6.0, -0.0, -0.5, -1.0, -1.5, -2.0, -3.0, -4.0, -6.0])


def pack_weight(w, fmt):
    k, n = w.shape
    w = f64(np.asarray(w, np.float32).astype(ml_dtypes.bfloat16)).reshape(k // 32, 32, n)
    amax = np.abs(w).max(1)
    if fmt == "e4m3":
        byte = np.frexp(amax)[1] - 1 + 127 - 7
    else:
        mant, ex = np.frexp(amax / 6.0)
        byte = np.where(mant > 0.5, ex, ex - 1) + 127
    byte = np.clip(np.where(amax > 0, byte, 1), 1, 254)
    scaled = (w * np.exp2(127.0 - byte)[:, None, :]).reshape(k, n).astype(np.float32)
    by_word = np.ascontiguousarray(scaled.reshape(k // 512, 128, 4, n).transpose(0, 1, 3, 2))
    if fmt == "e4m3":
        words = by_word.astype(ml_dtypes.float8_e4m3fn).view(np.uint8)
    else:
        c = by_word.astype(ml_dtypes.float4_e2m1fn).view(np.uint8) & 0xF
        words = (c[..., 0::2] | (c[..., 1::2] << 4)).reshape(k // 512, 128, 2 * n)
    return np.ascontiguousarray(words), np.ascontiguousarray(byte.astype(np.uint8).reshape(k // 512, 16, n))


def unpack_weight(words, scales, fmt):
    g, _, n = scales.shape
    words = np.ascontiguousarray(words).reshape(g, 128, n, -1)
    if fmt == "e4m3":
        vals = words.view(ml_dtypes.float8_e4m3fn).astype(np.float64)
    else:
        nib = np.empty((g, 128, n, 4), np.uint8)
        nib[..., 0::2] = words & 0xF
        nib[..., 1::2] = words >> 4
        vals = E2M1[nib]
    vals = vals * np.repeat(np.exp2(scales.astype(np.float64) - 127.0), 8, axis=1)[..., None]
    return vals.transpose(0, 1, 3, 2).reshape(g * 512, n)


D, E, T, I, G, Q = 512, 512, 2048, 512, 64, 128


def setup_inputs():
    n = np.random.standard_normal
    idx = np.random.permutation(T)[:I]
    fd = mx_kscale(D)
    fe = mx_kscale(E)
    fi = mx_kscale(I)
    ti = np.ones(T)
    ti[idx] = fi
    valsp = pack_weight(n((E, T)) / fe[:, None], "e4m3")
    return {
        "query": (n((D, Q)) * 0.7 / np.sqrt(D) * fd[:, None]).astype(np.float32),
        "keys": (n((D, T)) / fd[:, None]).astype(np.float32),
        "gout": (n((E, Q)) * 1 / np.sqrt(E) * fe[:, None]).astype(np.float32),
        "vals_words": valsp[0],
        "vals_scales": valsp[1],
        "keyrows": (n((D, T)) / ti).astype(np.float32),
        "fs": (np.random.uniform(0.5, 2.0, (1, I)) * fi).astype(np.float32),
        "res": (n((Q, D)) * 4.0).astype(np.float32),
        "offs": striped(idx),
    }


def reference(query, keys, gout, vals_words, vals_scales, keyrows, fs, res, offs):
    idx = unstriped(offs)
    valsu = unpack_weight(vals_words, vals_scales, "e4m3")
    queryq = mxq(f64(query), 0, "e4m3")
    keysidxq = mxq(f64(keys)[:, idx], 0, "e4m3")
    a = queryq.T @ keysidxq
    p = np.exp(a - np.max(a, axis=1, keepdims=True))
    zi = 1.0 / p.reshape(Q, G, I // G).sum(axis=2)
    zr = np.repeat(zi, I // G, axis=1)
    pn = p * zr
    goutq = mxq(f64(gout), 0, "e4m3")
    valsidxg = valsu[:, idx]
    dp = goutq.T @ valsidxg
    mg = (pn * dp).reshape(Q, G, I // G).sum(axis=2)
    mr = np.repeat(mg, I // G, axis=1)
    ds = pn * (dp - mr) * f64(fs)
    dt = ds.T
    kt = f64(keyrows)[:, idx].T
    dtq = mxq(dt, 0, "e4m3")
    ktq = mxq(kt, 0, "e4m3")
    gq = dtq.T @ ktq
    y = gq + f64(res)
    return y

@@ -1,0 +1,212 @@
+from contextlib import ExitStack
+
+import concourse.mybir as mybir
+from concourse.masks import make_identity
+
+D, E, T, I, G, Q = 512, 512, 2048, 512, 64, 128
+FLOPS = 2 * Q * I * (D + E + D)
+
+F32 = mybir.dt.float32
+BF16 = mybir.dt.bfloat16
+I32 = mybir.dt.int32
+U32 = mybir.dt.uint32
+U16 = mybir.dt.uint16
+U8 = mybir.dt.uint8
+FP8X4 = mybir.dt.float8_e4m3fn_x4
+ALU = mybir.AluOpType
+ACT = mybir.ActivationFunctionType
+AXIS = mybir.AxisListType
+
+P = 128
+PACK = 4
+HALVES = 2
+HI = I // HALVES
+HG = G // HALVES
+HS = P // HALVES
+BLOCKS = D // P
+SCALAR_BLOCK = 0
+
+
+def tile_attend_ggroupquery_kernel(tc, query, keys, gout, vals_words, vals_scales, keyrows, fs, res, offs, out):
+    nc = tc.nc
+    with ExitStack() as ctx:
+        sb = ctx.enter_context(tc.tile_pool(name="sb", bufs=1))
+        ps = ctx.enter_context(tc.psum_pool(name="ps", bufs=1))
+        ps2 = ctx.enter_context(tc.psum_pool(name="ps2", bufs=2))
+
+        def mx_tiles(name, width, tag=None):
+            codes = sb.tile([P, width], U32, name=name + "_codes", tag=tag or name + "_codes", align_bytes=64)
+            scales = sb.tile([P, width], U8, name=name + "_scales", align_bytes=64)
+            return codes, scales
+
+        def quantize(operand, cols, grouped):
+            codes, scales = operand
+            nc.vector.quantize_mx(out=codes[:, cols].bitcast(FP8X4), scales=scales[:, cols], in_=grouped)
+
+        def mx_product(acc, lhs, rhs, cols):
+            nc.tensor.matmul_mx(out=acc, lhsT=lhs[0][:].bitcast(FP8X4), lhsT_scale=lhs[1][:],
+                                rhs=rhs[0][:, cols].bitcast(FP8X4), rhs_scale=rhs[1][:, cols],
+                                start=True, stop=True)
+
+        offsets = sb.tile([P, I // 16], U16, name="offsets")
+        key_planes = [sb.tile([P, T], F32, name="keys%d" % t) for t in range(PACK)]
+        row_blocks = [sb.tile([P, T], F32, name="keyrows%d" % j, align_bytes=64) for j in range(BLOCKS)]
+        q_raw = sb.tile([P, PACK, Q], F32, name="q_raw")
+        g_raw = sb.tile([P, PACK, Q], F32, name="g_raw")
+        v_words = sb.tile([P, T], U32, name="vals_pool_words")
+        v_scales = sb.tile([P, T], U8, name="vals_pool_scales")
+        fs_col = sb.tile([P, PACK], F32, name="fs_col")
+        res_sb = sb.tile([P, D], F32, name="res_sb")
+        ident = sb.tile([P, P], F32, name="ident")
+
+        nc.vector.memset(v_scales[:].bitcast(I32), 0)
+        for quad in range(4):
+            nc.scalar.dma_start(out=v_scales[32 * quad:32 * quad + 4, :].bitcast(I32),
+                                in_=vals_scales[0, 4 * quad:4 * quad + 4, :].bitcast(I32))
+        nc.scalar.dma_start(out=fs_col[:], in_=fs.rearrange("o (p r) -> (o p) r", r=PACK))
+        make_identity(nc, ident[:])
+
+        keys_by_plane = keys.rearrange("(p t) c -> t p c", t=PACK)
+        nc.sync.dma_start(out=key_planes[0][:], in_=keys_by_plane[0])
+        nc.sync.dma_start(offsets[:], offs)
+        for t in range(1, PACK):
+            nc.sync.dma_start(out=key_planes[t][:], in_=keys_by_plane[t])
+        nc.sync.dma_start(out=q_raw[:], in_=query.rearrange("(p t) q -> p t q", t=PACK))
+        nc.sync.dma_start(out=g_raw[:], in_=gout.rearrange("(p t) q -> p t q", t=PACK))
+        nc.sync.dma_start(out=v_words[:].bitcast(I32),
+                          in_=vals_words[0].rearrange("p n t -> p (n t)").bitcast(I32))
+        for j in range(BLOCKS):
+            nc.sync.dma_start(out=row_blocks[j][:], in_=keyrows[j * P:(j + 1) * P, :])
+        nc.sync.dma_start(out=res_sb[:], in_=res)
+
+        half_cols = [slice(c * HI, (c + 1) * HI) for c in range(HALVES)]
+        half_offs = [offsets[:, c * HI // 16:(c + 1) * HI // 16] for c in range(HALVES)]
+
+        k_grouped = sb.tile([P, I, PACK], BF16, name="k_grouped", align_bytes=64)
+        v_scale_bytes = sb.tile([P, I], U8, name="v_scale_bytes", align_bytes=64)
+        nc.vector.tensor_copy(k_grouped[:, :, 0], key_planes[0][:].indirect(offsets[:]))
+        nc.vector.tensor_copy(v_scale_bytes[:], v_scales[:].indirect(offsets[:]))
+        for t in range(1, PACK - 1):
+            nc.vector.tensor_copy(k_grouped[:, :, t], key_planes[t][:].indirect(offsets[:]))
+        for c in range(HALVES):
+            nc.vector.tensor_copy(k_grouped[:, half_cols[c], PACK - 1], key_planes[PACK - 1][:].indirect(half_offs[c]))
+
+        q_grouped = sb.tile([P, Q, PACK], BF16, name="q_grouped", align_bytes=64)
+        g_grouped = sb.tile([P, Q, PACK], BF16, name="g_grouped", align_bytes=64)
+        nc.scalar.copy(out=q_grouped[:], in_=q_raw[:].rearrange("p t q -> p q t"))
+        nc.scalar.copy(out=g_grouped[:], in_=g_raw[:].rearrange("p t q -> p q t"))
+        q_mx = mx_tiles("q", Q)
+        g_mx = mx_tiles("g", Q)
+        k_mx = mx_tiles("k", I)
+        quantize(q_mx, slice(0, Q), q_grouped[:].rearrange("p q t -> p (q t)"))
+        a_ps = ps.tile([P, I], F32, name="a_ps")
+        for c in range(HALVES):
+            quantize(k_mx, half_cols[c], k_grouped[:, half_cols[c], :].rearrange("p i t -> p (i t)"))
+            mx_product(a_ps[:, half_cols[c]], q_mx, k_mx, half_cols[c])
+        quantize(g_mx, slice(0, Q), g_grouped[:].rearrange("p q t -> p (q t)"))
+
+        neg_max = sb.tile([P, 1], F32, name="neg_max")
+        nc.vector.tensor_reduce(out=neg_max[:], in_=a_ps[:], axis=AXIS.X, op=ALU.max, negate=True)
+
+        v_codes = sb.tile([P, I], U32, name="v_codes", tag="k_codes", align_bytes=64)
+        v_mx = (v_codes, v_scale_bytes)
+        nc.vector.tensor_copy(v_codes[:], v_words[:].indirect(offsets[:]))
+        dp_ps = ps.tile([P, I], F32, name="dp_ps")
+        mx_product(dp_ps[:], g_mx, v_mx, slice(0, I))
+
+        def paired(bank, c):
+            return bank[:, half_cols[c]].rearrange("p (s h e) -> p h s e", h=2, e=2)
+
+        def by_group(x):
+            return x.rearrange("p h (g s) e -> p g h (s e)", s=2)
+
+        def as_groups(x):
+            return x.rearrange("p h (g s) e -> p h g (s e)", s=2)
+
+        def spread(per_group):
+            return per_group[:].unsqueeze(1).unsqueeze(3).to_broadcast([P, 2, HG, 4])
+
+        halves = range(HALVES)
+        p_sb = [sb.tile([P, 2, HS, 2], F32, name="p%d" % c) for c in halves]
+        pn = [sb.tile([P, 2, HS, 2], F32, name="pn%d" % c) for c in halves]
+        sums_all = sb.tile([P, G], F32, name="sums_all", tag="vals_pool_words")
+        sums = [sums_all[:, c * HG:(c + 1) * HG] for c in halves]
+        zi = [sb.tile([P, HG], F32, name="zi%d" % c) for c in halves]
+        neg_mg = [sb.tile([P, HG], F32, name="neg_mg%d" % c) for c in halves]
+        pd_all = sb.tile([P, 2, P, 2], F32, name="pd_all")
+        pm_all = sb.tile([P, 2, P, 2], F32, name="pm_all")
+        pd = [pd_all[:, :, c * HS:(c + 1) * HS, :] for c in halves]
+        pm = [pm_all[:, :, c * HS:(c + 1) * HS, :] for c in halves]
+        for c in halves:
+            nc.scalar.activation(out=p_sb[c][:], in_=paired(a_ps, c), func=ACT.Exp, bias=neg_max[:], scale=1.0)
+        for c in halves:
+            nc.vector.tensor_reduce(out=sums[c], in_=by_group(p_sb[c][:]), axis=AXIS.XY, op=ALU.add)
+        for c in halves:
+            nc.vector.reciprocal(out=zi[c][:], in_=sums[c])
+        for c in halves:
+            nc.vector.tensor_tensor(out=as_groups(pn[c][:]), in0=as_groups(p_sb[c][:]), in1=spread(zi[c]), op=ALU.mult)
+        for c in halves:
+            nc.vector.tensor_tensor(out=pd[c], in0=pn[c][:], in1=paired(dp_ps, c), op=ALU.mult)
+        ds_ps = ps.tile([P, PACK, Q], F32, name="ds_ps")
+        for r in range(PACK):
+            nc.tensor.matmul(out=ds_ps[:, r, :], lhsT=pd_all[:, r // 2, :, r % 2], rhs=ident[:],
+                             is_transpose=True, start=(r == 0), stop=False)
+        for c in halves:
+            nc.vector.tensor_reduce(out=neg_mg[c][:], in_=by_group(pd[c]), axis=AXIS.XY, op=ALU.add, negate=True)
+        for c in halves:
+            nc.vector.tensor_tensor(out=as_groups(pm[c]), in0=as_groups(pn[c][:]), in1=spread(neg_mg[c]), op=ALU.mult)
+        for r in range(PACK):
+            nc.tensor.matmul(out=ds_ps[:, r, :], lhsT=pm_all[:, r // 2, :, r % 2], rhs=ident[:],
+                             is_transpose=True, start=False, stop=(r == PACK - 1))
+
+        pair_grouped = sb.tile([P, 2 * P, PACK], BF16, name="pair_grouped", align_bytes=64)
+        kt_grouped = [pair_grouped[:, :P, :], pair_grouped[:, P:, :]]
+        for j in (2, 3):
+            single = sb.tile([P, P, PACK], BF16, name="kt_grouped%d" % j, align_bytes=64)
+            kt_grouped.append(single[:])
+
+        def gather_and_turn(j):
+            picked = sb.tile([P, I], BF16, name="picked%d" % j)
+            if j == SCALAR_BLOCK:
+                rounded = sb.tile([P, T], BF16, name="rounded")
+                nc.scalar.activation(out=rounded[:], in_=row_blocks[j][:], func=ACT.Copy)
+                nc.scalar.activation(out=picked[:], in_=rounded[:].indirect(offsets[:]), func=ACT.Copy)
+            else:
+                nc.vector.tensor_copy(picked[:], row_blocks[j][:].indirect(offsets[:]))
+            words = picked[:].bitcast(F32)
+            turned = ps2.tile([P, 2, P], F32, name="turned")
+            for u in range(2):
+                nc.tensor.transpose(turned[:, u, :], words[:, u::2], ident[:])
+            nc.scalar.copy(out=kt_grouped[j].bitcast(F32), in_=turned[:].rearrange("p u d -> p d u"))
+
+        def quantize_rows(name, grouped, count, tag):
+            operand = mx_tiles(name, count * P, tag)
+            quantize(operand, slice(0, count * P), grouped.rearrange("p d r -> p (d r)"))
+            return operand
+
+        gather_and_turn(0)
+        gather_and_turn(1)
+
+        dt_grouped = sb.tile([P, Q, PACK], BF16, name="dt_grouped", tag="keyrows1", align_bytes=64)
+        dt_mx = mx_tiles("dt", Q)
+        nc.vector.tensor_tensor(out=dt_grouped[:], in0=ds_ps[:].rearrange("p r q -> p q r"),
+                                in1=fs_col[:].unsqueeze(1).to_broadcast([P, Q, PACK]), op=ALU.mult)
+        quantize(dt_mx, slice(0, Q), dt_grouped[:].rearrange("p q r -> p (q r)"))
+        gather_and_turn(2)
+        kt01 = quantize_rows("kt01", pair_grouped[:], 2, "keyrows2")
+        gather_and_turn(3)
+        kt2 = quantize_rows("kt2", kt_grouped[2], 1, "keyrows3")
+        kt3 = quantize_rows("kt3", kt_grouped[3], 1, None)
+
+        last = BLOCKS - 1
+        early_ps = ps.tile([P, last * P], F32, name="early_ps")
+        mx_product(early_ps[:, :2 * P], dt_mx, kt01, slice(0, 2 * P))
+        mx_product(early_ps[:, 2 * P:], dt_mx, kt2, slice(0, P))
+        late_ps = ps.tile([P, P], F32, name="late_ps")
+        mx_product(late_ps[:], dt_mx, kt3, slice(0, P))
+        early = sb.tile([P, last * P], F32, name="early")
+        nc.vector.tensor_tensor(out=early[:], in0=early_ps[:], in1=res_sb[:, :last * P], op=ALU.add)
+        nc.sync.dma_start(out=out[:, :last * P], in_=early[:])
+        late = sb.tile([P, P], F32, name="late")
+        nc.vector.tensor_tensor(out=late[:], in0=late_ps[:], in1=res_sb[:, last * P:], op=ALU.add)
+        nc.sync.dma_start(out=out[:, last * P:], in_=late[:])

@@ -187,15 +187,19 @@ def tile_attend_ggroupquery_kernel(tc, query, keys, gout, vals_words, vals_scale
         gather_and_turn(0)
         gather_and_turn(1)
 
-        dt_grouped = sb.tile([P, Q, PACK], BF16, name="dt_grouped", tag="keyrows1", align_bytes=64)
-        dt_mx = mx_tiles("dt", Q)
-        nc.vector.tensor_tensor(out=dt_grouped[:], in0=ds_ps[:].rearrange("p r q -> p q r"),
-                                in1=fs_col[:].unsqueeze(1).to_broadcast([P, Q, PACK]), op=ALU.mult)
-        quantize(dt_mx, slice(0, Q), dt_grouped[:].rearrange("p q r -> p (q r)"))
+        dt_grouped = sb.tile([P, Q, PACK], BF16, name="dt_grouped", align_bytes=64)
+        for r in range(PACK):
+            nc.scalar.activation(out=dt_grouped[:, :, r], in_=ds_ps[:, r, :], func=ACT.Copy, scale=fs_col[:, r:r + 1])
         gather_and_turn(2)
-        kt01 = quantize_rows("kt01", pair_grouped[:], 2, "keyrows2")
         gather_and_turn(3)
-        kt2 = quantize_rows("kt2", kt_grouped[2], 1, "keyrows3")
+        late_codes = sb.tile([P, D], U32, name="late_codes", tag="keyrows3", align_bytes=64)
+        late_scales = sb.tile([P, D], U8, name="late_scales", align_bytes=64)
+        dt_mx = (late_codes[:, :P], late_scales[:, :P])
+        kt01 = (late_codes[:, P:3 * P], late_scales[:, P:3 * P])
+        kt2 = (late_codes[:, 3 * P:], late_scales[:, 3 * P:])
+        quantize(dt_mx, slice(0, Q), dt_grouped[:].rearrange("p q r -> p (q r)"))
+        quantize(kt01, slice(0, 2 * P), pair_grouped[:].rearrange("p d r -> p (d r)"))
+        quantize(kt2, slice(0, P), kt_grouped[2].rearrange("p d r -> p (d r)"))
         kt3 = quantize_rows("kt3", kt_grouped[3], 1, None)
 
         last = BLOCKS - 1

from contextlib import ExitStack

import concourse.mybir as mybir
from concourse.masks import make_identity

D, E, T, I, G, Q = 512, 512, 2048, 512, 64, 128
FLOPS = 2 * Q * I * (D + E + D)

F32 = mybir.dt.float32
BF16 = mybir.dt.bfloat16
I32 = mybir.dt.int32
U32 = mybir.dt.uint32
U16 = mybir.dt.uint16
U8 = mybir.dt.uint8
FP8X4 = mybir.dt.float8_e4m3fn_x4
ALU = mybir.AluOpType
ACT = mybir.ActivationFunctionType
AXIS = mybir.AxisListType

P = 128
PACK = 4
HALVES = 2
HI = I // HALVES
HG = G // HALVES
HS = P // HALVES
BLOCKS = D // P
SCALAR_BLOCK = 0


def tile_attend_ggroupquery_kernel(tc, query, keys, gout, vals_words, vals_scales, keyrows, fs, res, offs, out):
    nc = tc.nc
    with ExitStack() as ctx:
        sb = ctx.enter_context(tc.tile_pool(name="sb", bufs=1))
        ps = ctx.enter_context(tc.psum_pool(name="ps", bufs=1))
        ps2 = ctx.enter_context(tc.psum_pool(name="ps2", bufs=2))

        def mx_tiles(name, width, tag=None):
            codes = sb.tile([P, width], U32, name=name + "_codes", tag=tag or name + "_codes", align_bytes=64)
            scales = sb.tile([P, width], U8, name=name + "_scales", align_bytes=64)
            return codes, scales

        def quantize(operand, cols, grouped):
            codes, scales = operand
            nc.vector.quantize_mx(out=codes[:, cols].bitcast(FP8X4), scales=scales[:, cols], in_=grouped)

        def mx_product(acc, lhs, rhs, cols):
            nc.tensor.matmul_mx(out=acc, lhsT=lhs[0][:].bitcast(FP8X4), lhsT_scale=lhs[1][:],
                                rhs=rhs[0][:, cols].bitcast(FP8X4), rhs_scale=rhs[1][:, cols],
                                start=True, stop=True)

        offsets = sb.tile([P, I // 16], U16, name="offsets")
        key_planes = [sb.tile([P, T], F32, name="keys%d" % t) for t in range(PACK)]
        row_blocks = [sb.tile([P, T], F32, name="keyrows%d" % j, align_bytes=64) for j in range(BLOCKS)]
        q_raw = sb.tile([P, PACK, Q], F32, name="q_raw")
        g_raw = sb.tile([P, PACK, Q], F32, name="g_raw")
        v_words = sb.tile([P, T], U32, name="vals_pool_words")
        v_scales = sb.tile([P, T], U8, name="vals_pool_scales")
        fs_col = sb.tile([P, PACK], F32, name="fs_col")
        res_sb = sb.tile([P, D], F32, name="res_sb")
        ident = sb.tile([P, P], F32, name="ident")

        nc.vector.memset(v_scales[:].bitcast(I32), 0)
        for quad in range(4):
            nc.scalar.dma_start(out=v_scales[32 * quad:32 * quad + 4, :].bitcast(I32),
                                in_=vals_scales[0, 4 * quad:4 * quad + 4, :].bitcast(I32))
        nc.scalar.dma_start(out=fs_col[:], in_=fs.rearrange("o (p r) -> (o p) r", r=PACK))
        make_identity(nc, ident[:])

        keys_by_plane = keys.rearrange("(p t) c -> t p c", t=PACK)
        nc.sync.dma_start(out=key_planes[0][:], in_=keys_by_plane[0])
        nc.sync.dma_start(offsets[:], offs)
        for t in range(1, PACK):
            nc.sync.dma_start(out=key_planes[t][:], in_=keys_by_plane[t])
        nc.sync.dma_start(out=q_raw[:], in_=query.rearrange("(p t) q -> p t q", t=PACK))
        nc.sync.dma_start(out=g_raw[:], in_=gout.rearrange("(p t) q -> p t q", t=PACK))
        nc.sync.dma_start(out=v_words[:].bitcast(I32),
                          in_=vals_words[0].rearrange("p n t -> p (n t)").bitcast(I32))
        for j in range(BLOCKS):
            nc.sync.dma_start(out=row_blocks[j][:], in_=keyrows[j * P:(j + 1) * P, :])
        nc.sync.dma_start(out=res_sb[:], in_=res)

        half_cols = [slice(c * HI, (c + 1) * HI) for c in range(HALVES)]
        half_offs = [offsets[:, c * HI // 16:(c + 1) * HI // 16] for c in range(HALVES)]

        k_grouped = sb.tile([P, I, PACK], BF16, name="k_grouped", align_bytes=64)
        v_scale_bytes = sb.tile([P, I], U8, name="v_scale_bytes", align_bytes=64)
        nc.vector.tensor_copy(k_grouped[:, :, 0], key_planes[0][:].indirect(offsets[:]))
        nc.vector.tensor_copy(v_scale_bytes[:], v_scales[:].indirect(offsets[:]))
        for t in range(1, PACK - 1):
            nc.vector.tensor_copy(k_grouped[:, :, t], key_planes[t][:].indirect(offsets[:]))
        for c in range(HALVES):
            nc.vector.tensor_copy(k_grouped[:, half_cols[c], PACK - 1], key_planes[PACK - 1][:].indirect(half_offs[c]))

        q_grouped = sb.tile([P, Q, PACK], BF16, name="q_grouped", align_bytes=64)
        g_grouped = sb.tile([P, Q, PACK], BF16, name="g_grouped", align_bytes=64)
        nc.scalar.copy(out=q_grouped[:], in_=q_raw[:].rearrange("p t q -> p q t"))
        nc.scalar.copy(out=g_grouped[:], in_=g_raw[:].rearrange("p t q -> p q t"))
        q_mx = mx_tiles("q", Q)
        g_mx = mx_tiles("g", Q)
        k_mx = mx_tiles("k", I)
        quantize(q_mx, slice(0, Q), q_grouped[:].rearrange("p q t -> p (q t)"))
        a_ps = ps.tile([P, I], F32, name="a_ps")
        for c in range(HALVES):
            quantize(k_mx, half_cols[c], k_grouped[:, half_cols[c], :].rearrange("p i t -> p (i t)"))
            mx_product(a_ps[:, half_cols[c]], q_mx, k_mx, half_cols[c])
        quantize(g_mx, slice(0, Q), g_grouped[:].rearrange("p q t -> p (q t)"))

        neg_max = sb.tile([P, 1], F32, name="neg_max")
        nc.vector.tensor_reduce(out=neg_max[:], in_=a_ps[:], axis=AXIS.X, op=ALU.max, negate=True)

        v_codes = sb.tile([P, I], U32, name="v_codes", tag="k_codes", align_bytes=64)
        v_mx = (v_codes, v_scale_bytes)
        nc.vector.tensor_copy(v_codes[:], v_words[:].indirect(offsets[:]))
        dp_ps = ps.tile([P, I], F32, name="dp_ps")
        mx_product(dp_ps[:], g_mx, v_mx, slice(0, I))

        def paired(bank, c):
            return bank[:, half_cols[c]].rearrange("p (s h e) -> p h s e", h=2, e=2)

        def by_group(x):
            return x.rearrange("p h (g s) e -> p g h (s e)", s=2)

        def as_groups(x):
            return x.rearrange("p h (g s) e -> p h g (s e)", s=2)

        def spread(per_group):
            return per_group[:].unsqueeze(1).unsqueeze(3).to_broadcast([P, 2, HG, 4])

        halves = range(HALVES)
        p_sb = [sb.tile([P, 2, HS, 2], F32, name="p%d" % c) for c in halves]
        pn = [sb.tile([P, 2, HS, 2], F32, name="pn%d" % c) for c in halves]
        sums_all = sb.tile([P, G], F32, name="sums_all", tag="vals_pool_words")
        sums = [sums_all[:, c * HG:(c + 1) * HG] for c in halves]
        zi = [sb.tile([P, HG], F32, name="zi%d" % c) for c in halves]
        neg_mg = [sb.tile([P, HG], F32, name="neg_mg%d" % c) for c in halves]
        pd_all = sb.tile([P, 2, P, 2], F32, name="pd_all")
        pm_all = sb.tile([P, 2, P, 2], F32, name="pm_all")
        pd = [pd_all[:, :, c * HS:(c + 1) * HS, :] for c in halves]
        pm = [pm_all[:, :, c * HS:(c + 1) * HS, :] for c in halves]
        for c in halves:
            nc.scalar.activation(out=p_sb[c][:], in_=paired(a_ps, c), func=ACT.Exp, bias=neg_max[:], scale=1.0)
        for c in halves:
            nc.vector.tensor_reduce(out=sums[c], in_=by_group(p_sb[c][:]), axis=AXIS.XY, op=ALU.add)
        for c in halves:
            nc.vector.reciprocal(out=zi[c][:], in_=sums[c])
        for c in halves:
            nc.vector.tensor_tensor(out=as_groups(pn[c][:]), in0=as_groups(p_sb[c][:]), in1=spread(zi[c]), op=ALU.mult)
        for c in halves:
            nc.vector.tensor_tensor(out=pd[c], in0=pn[c][:], in1=paired(dp_ps, c), op=ALU.mult)
        ds_ps = ps.tile([P, PACK, Q], F32, name="ds_ps")
        for r in range(PACK):
            nc.tensor.matmul(out=ds_ps[:, r, :], lhsT=pd_all[:, r // 2, :, r % 2], rhs=ident[:],
                             is_transpose=True, start=(r == 0), stop=False)
        for c in halves:
            nc.vector.tensor_reduce(out=neg_mg[c][:], in_=by_group(pd[c]), axis=AXIS.XY, op=ALU.add, negate=True)
        for c in halves:
            nc.vector.tensor_tensor(out=as_groups(pm[c]), in0=as_groups(pn[c][:]), in1=spread(neg_mg[c]), op=ALU.mult)
        for r in range(PACK):
            nc.tensor.matmul(out=ds_ps[:, r, :], lhsT=pm_all[:, r // 2, :, r % 2], rhs=ident[:],
                             is_transpose=True, start=False, stop=(r == PACK - 1))

        pair_grouped = sb.tile([P, 2 * P, PACK], BF16, name="pair_grouped", align_bytes=64)
        kt_grouped = [pair_grouped[:, :P, :], pair_grouped[:, P:, :]]
        for j in (2, 3):
            single = sb.tile([P, P, PACK], BF16, name="kt_grouped%d" % j, align_bytes=64)
            kt_grouped.append(single[:])

        def gather_and_turn(j):
            picked = sb.tile([P, I], BF16, name="picked%d" % j)
            if j == SCALAR_BLOCK:
                rounded = sb.tile([P, T], BF16, name="rounded")
                nc.scalar.activation(out=rounded[:], in_=row_blocks[j][:], func=ACT.Copy)
                nc.scalar.activation(out=picked[:], in_=rounded[:].indirect(offsets[:]), func=ACT.Copy)
            else:
                nc.vector.tensor_copy(picked[:], row_blocks[j][:].indirect(offsets[:]))
            words = picked[:].bitcast(F32)
            turned = ps2.tile([P, 2, P], F32, name="turned")
            for u in range(2):
                nc.tensor.transpose(turned[:, u, :], words[:, u::2], ident[:])
            nc.scalar.copy(out=kt_grouped[j].bitcast(F32), in_=turned[:].rearrange("p u d -> p d u"))

        def quantize_rows(name, grouped, count, tag):
            operand = mx_tiles(name, count * P, tag)
            quantize(operand, slice(0, count * P), grouped.rearrange("p d r -> p (d r)"))
            return operand

        gather_and_turn(0)
        gather_and_turn(1)

        dt_grouped = sb.tile([P, Q, PACK], BF16, name="dt_grouped", align_bytes=64)
        for r in range(PACK):
            nc.scalar.activation(out=dt_grouped[:, :, r], in_=ds_ps[:, r, :], func=ACT.Copy, scale=fs_col[:, r:r + 1])
        gather_and_turn(2)
        gather_and_turn(3)
        late_codes = sb.tile([P, D], U32, name="late_codes", tag="keyrows3", align_bytes=64)
        late_scales = sb.tile([P, D], U8, name="late_scales", align_bytes=64)
        dt_mx = (late_codes[:, :P], late_scales[:, :P])
        kt01 = (late_codes[:, P:3 * P], late_scales[:, P:3 * P])
        kt2 = (late_codes[:, 3 * P:], late_scales[:, 3 * P:])
        quantize(dt_mx, slice(0, Q), dt_grouped[:].rearrange("p q r -> p (q r)"))
        quantize(kt01, slice(0, 2 * P), pair_grouped[:].rearrange("p d r -> p (d r)"))
        quantize(kt2, slice(0, P), kt_grouped[2].rearrange("p d r -> p (d r)"))
        kt3 = quantize_rows("kt3", kt_grouped[3], 1, None)

        last = BLOCKS - 1
        early_ps = ps.tile([P, last * P], F32, name="early_ps")
        mx_product(early_ps[:, :2 * P], dt_mx, kt01, slice(0, 2 * P))
        mx_product(early_ps[:, 2 * P:], dt_mx, kt2, slice(0, P))
        late_ps = ps.tile([P, P], F32, name="late_ps")
        mx_product(late_ps[:], dt_mx, kt3, slice(0, P))
        early = sb.tile([P, last * P], F32, name="early")
        nc.vector.tensor_tensor(out=early[:], in0=early_ps[:], in1=res_sb[:, :last * P], op=ALU.add)
        nc.sync.dma_start(out=out[:, :last * P], in_=early[:])
        late = sb.tile([P, P], F32, name="late")
        nc.vector.tensor_tensor(out=late[:], in0=late_ps[:], in1=res_sb[:, last * P:], op=ALU.add)
        nc.sync.dma_start(out=out[:, last * P:], in_=late[:])
